import numpy as np
import ml_dtypes


def mxq(x, axis, fmt="e4m3"):
    dtype, down = {"e4m3": (ml_dtypes.float8_e4m3fn, 7), "e5m2": (ml_dtypes.float8_e5m2, 14)}[fmt]
    v = np.moveaxis(np.asarray(x, np.float32).astype(ml_dtypes.bfloat16).astype(np.float64), axis, -1)
    blocks = v.reshape(v.shape[:-1] + (-1, 32))
    amax = np.abs(blocks).max(-1, keepdims=True)
    byte = np.maximum(np.where(amax > 0, np.frexp(amax)[1] - 1 + 127, 0) - down, 1)
    scale = np.exp2(byte - 127.0)
    codes = (blocks / scale).astype(np.float32).astype(dtype).astype(np.float64)
    return np.moveaxis((codes * scale).reshape(v.shape), -1, axis)


WIDE = False


def mx_kscale(k):
    if not WIDE:
        return np.ones(k)
    levels = np.array([10, -10, 5, -5, 0])
    if k % 512:
        return np.exp2(np.random.permutation(np.resize(levels, k // 32))).repeat(32)
    a = np.empty((k // 512, 16))
    for p in range(k // 512):
        a[p, :8] = np.random.permutation(np.resize(levels, 8))
        for g in range(8):
            far = levels[np.abs(levels - a[p, g]) >= 10]
            a[p, g + 8] = far[np.random.randint(len(far))]
    return np.exp2(a.ravel()).repeat(32)


def f64(x):
    return np.asarray(x).astype(np.float64)


def striped8(idx):
    return np.asarray(idx).reshape(8, -1, 16).transpose(0, 2, 1).reshape(128, -1).astype(np.uint16)


def unstriped8(offs):
    return offs.reshape(8, 16, -1).transpose(0, 2, 1).reshape(8, -1).astype(np.int64)


def pick8(x, idx, run):
    r = np.arange(len(x))
    return x[r[:, None], idx[r % (8 * run) // run]]


E2M1 = np.array([0.0, 0.5, 1.0, 1.5, 2.0, 3.0, 4.0, 6.0, -0.0, -0.5, -1.0, -1.5, -2.0, -3.0, -4.0, -6.0])


def pack_weight(w, fmt):
    k, n = w.shape
    w = f64(np.asarray(w, np.float32).astype(ml_dtypes.bfloat16)).reshape(k // 32, 32, n)
    amax = np.abs(w).max(1)
    if fmt == "e4m3":
        byte = np.frexp(amax)[1] - 1 + 127 - 7
    else:
        mant, ex = np.frexp(amax / 6.0)
        byte = np.where(mant > 0.5, ex, ex - 1) + 127
    byte = np.clip(np.where(amax > 0, byte, 1), 1, 254)
    scaled = (w * np.exp2(127.0 - byte)[:, None, :]).reshape(k, n).astype(np.float32)
    by_word = np.ascontiguousarray(scaled.reshape(k // 512, 128, 4, n).transpose(0, 1, 3, 2))
    if fmt == "e4m3":
        words = by_word.astype(ml_dtypes.float8_e4m3fn).view(np.uint8)
    else:
        c = by_word.astype(ml_dtypes.float4_e2m1fn).view(np.uint8) & 0xF
        words = (c[..., 0::2] | (c[..., 1::2] << 4)).reshape(k // 512, 128, 2 * n)
    return np.ascontiguousarray(words), np.ascontiguousarray(byte.astype(np.uint8).reshape(k // 512, 16, n))


def unpack_weight(words, scales, fmt):
    g, _, n = scales.shape
    words = np.ascontiguousarray(words).reshape(g, 128, n, -1)
    if fmt == "e4m3":
        vals = words.view(ml_dtypes.float8_e4m3fn).astype(np.float64)
    else:
        nib = np.empty((g, 128, n, 4), np.uint8)
        nib[..., 0::2] = words & 0xF
        nib[..., 1::2] = words >> 4
        vals = E2M1[nib]
    vals = vals * np.repeat(np.exp2(scales.astype(np.float64) - 127.0), 8, axis=1)[..., None]
    return vals.transpose(0, 1, 3, 2).reshape(g * 512, n)


D, T, I, Q = 512, 1024, 512, 128


def setup_inputs():
    n = np.random.standard_normal
    idx = np.stack([np.random.permutation(T)[:I] for _ in range(8)])
    idx2 = np.stack([np.random.permutation(T)[:I] for _ in range(8)])
    idx3 = np.stack([np.random.permutation(T)[:I] for _ in range(8)])
    fd = mx_kscale(D)
    keysp = pack_weight(n((D, T)) / fd[:, None], "e4m3")
    tagsp = pack_weight(n((D, T)) / fd[:, None], "e2m1")
    return {
        "query": (n((D, Q)) * 0.75 / np.sqrt(D) * fd[:, None]).astype(np.float32),
        "query2": (n((D, Q)) * 0.75 / np.sqrt(D) * fd[:, None]).astype(np.float32),
        "keys_words": keysp[0],
        "keys_scales": keysp[1],
        "tags_words": tagsp[0],
        "tags_scales": tagsp[1],
        "offs": striped8(idx),
        "offs2": striped8(idx2),
        "offs3": striped8(idx3),
    }


def reference(query, query2, keys_words, keys_scales, tags_words, tags_scales, offs, offs2, offs3):
    idx = unstriped8(offs)
    idx2 = unstriped8(offs2)
    idx3 = unstriped8(offs3)
    keysu = unpack_weight(keys_words, keys_scales, "e4m3")
    tagsu = unpack_weight(tags_words, tags_scales, "e2m1")
    queryq = mxq(f64(query), 0, "e4m3")
    query2q = mxq(f64(query2), 0, "e4m3")
    a = queryq.T @ keysu + query2q.T @ tagsu
    r = pick8(a, idx2, 16) - pick8(a, idx, 16)
    f1 = np.zeros((Q, T))
    f1[np.arange(Q)[:, None], idx[np.arange(Q) % 128 // 16]] = r
    f2 = np.zeros((Q, T))
    f2[np.arange(Q)[:, None], idx2[np.arange(Q) % 128 // 16]] = r
    c1 = a + f1
    c2 = c1 - f2
    y = pick8(c2, idx3, 16)
    return y

@@ -1,0 +1,173 @@
+from contextlib import ExitStack
+
+import concourse.mybir as mybir
+from concourse.masks import make_identity
+
+D, T, I, Q = 512, 1024, 512, 128
+FLOPS = 2 * 2 * D * Q * T
+
+F32 = mybir.dt.float32
+BF16 = mybir.dt.bfloat16
+I32 = mybir.dt.int32
+U32 = mybir.dt.uint32
+U16 = mybir.dt.uint16
+U8 = mybir.dt.uint8
+FP8X4 = mybir.dt.float8_e4m3fn_x4
+FP4X4 = mybir.dt.float4_e2m1fn_x4
+ADD = mybir.AluOpType.add
+SUB = mybir.AluOpType.subtract
+MULT = mybir.AluOpType.mult
+COPY = mybir.ActivationFunctionType.Copy
+
+P = 128
+PACK = 4
+HALF_T = T // 2
+HALF_I = I // 2
+LIST_COLS = I // 16
+HALF_LIST = LIST_COLS // 2
+TOKEN_RUNS = ((0, 512), (512, 768), (768, 1024))
+
+
+def tile_attend_swapped_parts_kernel(
+    tc, query, query2, keys_words, keys_scales, tags_words, tags_scales, offs, offs2, offs3, out
+):
+    nc = tc.nc
+    with ExitStack() as ctx:
+        sb = ctx.enter_context(tc.tile_pool(name="sb", bufs=1))
+        ps = ctx.enter_context(tc.psum_pool(name="ps", bufs=1))
+
+        tags_plane = sb.tile([P, T], U8, name="tags_plane", align_bytes=64)
+        keys_plane = sb.tile([P, T], U8, name="keys_plane", align_bytes=64)
+
+        def load_scales(plane, scales):
+            for quad in range(4):
+                nc.scalar.dma_start(
+                    out=plane[32 * quad : 32 * quad + 4, :].bitcast(I32),
+                    in_=scales[0, 4 * quad : 4 * quad + 4, :].bitcast(I32),
+                )
+
+        load_scales(tags_plane, tags_scales)
+        raw2 = sb.tile([P, PACK, Q], F32, name="raw2")
+        raw1 = sb.tile([P, PACK, Q], F32, name="raw1")
+        nc.sync.dma_start(out=raw2[:], in_=query2.rearrange("(p j) w -> p j w", j=PACK))
+        tags = sb.tile([P, 2 * T], U8, name="tags", align_bytes=64)
+        nc.sync.dma_start(out=tags[:].bitcast(I32), in_=tags_words[0].bitcast(I32))
+        nc.sync.dma_start(out=raw1[:], in_=query.rearrange("(p j) w -> p j w", j=PACK))
+        keys_flat = keys_words[0].rearrange("p n t -> p (n t)")
+        keys = [sb.tile([P, HALF_T], U32, name="keys%d" % h, align_bytes=64) for h in range(2)]
+        nc.sync.dma_start(out=keys[0][:].bitcast(I32), in_=keys_flat[:, : 4 * HALF_T].bitcast(I32))
+        load_scales(keys_plane, keys_scales)
+        nc.sync.dma_start(out=keys[1][:].bitcast(I32), in_=keys_flat[:, 4 * HALF_T :].bitcast(I32))
+        list1 = sb.tile([P, LIST_COLS], U16, name="list1")
+        list2 = sb.tile([P, LIST_COLS], U16, name="list2")
+        list3 = sb.tile([P, LIST_COLS], U16, name="list3")
+        nc.sync.dma_start(list1[:], offs)
+        nc.sync.dma_start(list2[:], offs2)
+        nc.sync.dma_start(list3[:], offs3)
+
+        f1 = [sb.tile([P, T], F32, name="f1_%d" % s) for s in range(2)]
+        for part in f1:
+            nc.vector.memset(part[:], 0.0)
+
+        grouped2 = sb.tile([P, Q, PACK], BF16, name="grouped2", align_bytes=64)
+        grouped1 = sb.tile([P, Q, PACK], BF16, name="grouped1", tag="grouped1_f2", align_bytes=64)
+        codes2 = sb.tile([P, Q], U32, name="codes2", align_bytes=64)
+        codes1 = sb.tile([P, Q], U32, name="codes1", align_bytes=64)
+        plane2 = sb.tile([P, Q], U8, name="plane2", align_bytes=64)
+        plane1 = sb.tile([P, Q], U8, name="plane1", align_bytes=64)
+        for raw, grouped, codes, plane in ((raw2, grouped2, codes2, plane2), (raw1, grouped1, codes1, plane1)):
+            nc.vector.tensor_copy(out=grouped[:], in_=raw[:].rearrange("p j w -> p w j"))
+            nc.vector.quantize_mx(
+                out=codes[:].bitcast(FP8X4),
+                scales=plane[:],
+                in_=grouped[:].rearrange("p w j -> p (w j)"),
+            )
+
+        f2 = sb.tile([P, T], F32, name="f2", tag="grouped1_f2", align_bytes=64)
+        nc.vector.memset(f2[:], 0.0)
+
+        banks = [ps.tile([P, hi - lo], F32, name="bank%d" % lo) for lo, hi in TOKEN_RUNS]
+        for bank, (lo, hi) in zip(banks, TOKEN_RUNS):
+            nc.tensor.matmul_mx(
+                out=bank[:],
+                lhsT=codes2[:].bitcast(FP8X4),
+                lhsT_scale=plane2[:],
+                rhs=tags[:, 2 * lo : 2 * hi].bitcast(FP4X4),
+                rhs_scale=tags_plane[:, lo:hi],
+                start=True,
+                stop=False,
+            )
+        a = sb.tile([P, T], F32, name="a")
+        for bank, (lo, hi) in zip(banks, TOKEN_RUNS):
+            half = lo // HALF_T
+            nc.tensor.matmul_mx(
+                out=bank[:],
+                lhsT=codes1[:].bitcast(FP8X4),
+                lhsT_scale=plane1[:],
+                rhs=keys[half][:, lo - half * HALF_T : hi - half * HALF_T].bitcast(FP8X4),
+                rhs_scale=keys_plane[:, lo:hi],
+                start=False,
+                stop=True,
+            )
+            if half == 0:
+                nc.scalar.copy(out=a[:, lo:hi], in_=bank[:])
+            else:
+                nc.vector.tensor_copy(out=a[:, lo:hi], in_=bank[:])
+
+        ident = sb.tile([P, P], F32, name="ident")
+        make_identity(nc, ident[:])
+        turned = [ps.tile([P, HALF_T], F32, name="turned%d" % h) for h in range(2)]
+        turned_sb = []
+        for h in range(2):
+            for b in range(4):
+                col = h * HALF_T + b * P
+                nc.tensor.matmul(
+                    turned[h][:, b * P : (b + 1) * P], a[:, col : col + P], ident[:],
+                    start=(b == 0), stop=False, is_transpose=True,
+                )
+
+        at2 = sb.tile([P, I], F32, name="at2")
+        minus_at1 = sb.tile([P, I], F32, name="minus_at1")
+        s0, s1 = slice(0, HALF_I), slice(HALF_I, I)
+        l0, l1 = slice(0, HALF_LIST), slice(HALF_LIST, LIST_COLS)
+        nc.vector.tensor_scalar(minus_at1[:, s0], a[:].indirect(list1[:, l0]), -1.0, 0.0, MULT, ADD)
+        nc.scalar.activation(at2[:, s0], a[:].indirect(list2[:, l0]), COPY)
+        nc.vector.tensor_tensor(f1[0][:].indirect(list1[:, l0]), at2[:, s0], minus_at1[:, s0], ADD)
+        nc.scalar.activation(at2[:, s1], a[:].indirect(list2[:, l1]), COPY)
+        nc.scalar.activation(minus_at1[:, s1], a[:].indirect(list1[:, l1]), COPY, scale=-1.0)
+        nc.vector.tensor_tensor(f1[1][:].indirect(list1[:, l1]), at2[:, s1], minus_at1[:, s1], ADD)
+        nc.vector.tensor_tensor(f2[:].indirect(list2[:]), at2[:], minus_at1[:], ADD)
+
+        c1 = [ps.tile([P, HALF_T], F32, name="c1_%d" % h) for h in range(2)]
+        for h in range(2):
+            for b in range(4):
+                col = h * HALF_T + b * P
+                nc.tensor.matmul(
+                    turned[h][:, b * P : (b + 1) * P], f1[0][:, col : col + P], ident[:],
+                    start=False, stop=False, is_transpose=True,
+                )
+        for h in range(2):
+            for b in range(4):
+                col = h * HALF_T + b * P
+                nc.tensor.matmul(
+                    turned[h][:, b * P : (b + 1) * P], f1[1][:, col : col + P], ident[:],
+                    start=False, stop=(b == 3), is_transpose=True,
+                )
+            c1_turned = sb.tile([P, HALF_T], F32, name="c1_turned%d" % h)
+            nc.scalar.copy(out=c1_turned[:], in_=turned[h][:])
+            turned_sb.append(c1_turned)
+        for h in range(2):
+            for b in range(4):
+                nc.tensor.transpose(c1[h][:, b * P : (b + 1) * P], turned_sb[h][:, b * P : (b + 1) * P], ident[:])
+
+        c2 = sb.tile([P, T], F32, name="c2")
+        for h in range(2):
+            cols = slice(h * HALF_T, (h + 1) * HALF_T)
+            nc.vector.tensor_tensor(c2[:, cols], c1[h][:], f2[:, cols], SUB)
+
+        res0 = sb.tile([P, HALF_I], F32, name="res0")
+        res1 = sb.tile([P, HALF_I], F32, name="res1")
+        nc.vector.tensor_copy(res0[:], c2[:].indirect(list3[:, l0]))
+        nc.scalar.activation(res1[:], c2[:].indirect(list3[:, l1]), COPY)
+        nc.sync.dma_start(out=out[:, s0], in_=res0[:])
+        nc.scalar.dma_start(out=out[:, s1], in_=res1[:])

@@ -25,7 +25,7 @@ HALF_T = T // 2
 HALF_I = I // 2
 LIST_COLS = I // 16
 HALF_LIST = LIST_COLS // 2
-TOKEN_RUNS = ((0, 512), (512, 768), (768, 1024))
+TOKEN_RUNS = ((0, 512), (512, 768), (768, 896), (896, 1024))
 
 
 def tile_attend_swapped_parts_kernel(
@@ -39,14 +39,14 @@ def tile_attend_swapped_parts_kernel(
         tags_plane = sb.tile([P, T], U8, name="tags_plane", align_bytes=64)
         keys_plane = sb.tile([P, T], U8, name="keys_plane", align_bytes=64)
 
-        def load_scales(plane, scales):
+        def load_scales(queue, plane, scales):
             for quad in range(4):
-                nc.scalar.dma_start(
+                queue.dma_start(
                     out=plane[32 * quad : 32 * quad + 4, :].bitcast(I32),
                     in_=scales[0, 4 * quad : 4 * quad + 4, :].bitcast(I32),
                 )
 
-        load_scales(tags_plane, tags_scales)
+        load_scales(nc.scalar, tags_plane, tags_scales)
         raw2 = sb.tile([P, PACK, Q], F32, name="raw2")
         raw1 = sb.tile([P, PACK, Q], F32, name="raw1")
         nc.sync.dma_start(out=raw2[:], in_=query2.rearrange("(p j) w -> p j w", j=PACK))
@@ -54,10 +54,9 @@ def tile_attend_swapped_parts_kernel(
         nc.sync.dma_start(out=tags[:].bitcast(I32), in_=tags_words[0].bitcast(I32))
         nc.sync.dma_start(out=raw1[:], in_=query.rearrange("(p j) w -> p j w", j=PACK))
         keys_flat = keys_words[0].rearrange("p n t -> p (n t)")
-        keys = [sb.tile([P, HALF_T], U32, name="keys%d" % h, align_bytes=64) for h in range(2)]
-        nc.sync.dma_start(out=keys[0][:].bitcast(I32), in_=keys_flat[:, : 4 * HALF_T].bitcast(I32))
-        load_scales(keys_plane, keys_scales)
-        nc.sync.dma_start(out=keys[1][:].bitcast(I32), in_=keys_flat[:, 4 * HALF_T :].bitcast(I32))
+        keys = sb.tile([P, T], U32, name="keys", align_bytes=64)
+        nc.sync.dma_start(out=keys[:].bitcast(I32), in_=keys_flat.bitcast(I32))
+        load_scales(nc.sync, keys_plane, keys_scales)
         list1 = sb.tile([P, LIST_COLS], U16, name="list1")
         list2 = sb.tile([P, LIST_COLS], U16, name="list2")
         list3 = sb.tile([P, LIST_COLS], U16, name="list3")
@@ -98,18 +97,17 @@ def tile_attend_swapped_parts_kernel(
                 stop=False,
             )
         a = sb.tile([P, T], F32, name="a")
-        for bank, (lo, hi) in zip(banks, TOKEN_RUNS):
-            half = lo // HALF_T
+        for run, (bank, (lo, hi)) in enumerate(zip(banks, TOKEN_RUNS)):
             nc.tensor.matmul_mx(
                 out=bank[:],
                 lhsT=codes1[:].bitcast(FP8X4),
                 lhsT_scale=plane1[:],
-                rhs=keys[half][:, lo - half * HALF_T : hi - half * HALF_T].bitcast(FP8X4),
+                rhs=keys[:, lo:hi].bitcast(FP8X4),
                 rhs_scale=keys_plane[:, lo:hi],
                 start=False,
                 stop=True,
             )
-            if half == 0:
+            if run % 2 == 0:
                 nc.scalar.copy(out=a[:, lo:hi], in_=bank[:])
             else:
                 nc.vector.tensor_copy(out=a[:, lo:hi], in_=bank[:])

@@ -39,24 +39,24 @@ def tile_attend_swapped_parts_kernel(
         tags_plane = sb.tile([P, T], U8, name="tags_plane", align_bytes=64)
         keys_plane = sb.tile([P, T], U8, name="keys_plane", align_bytes=64)
 
-        def load_scales(queue, plane, scales):
-            for quad in range(4):
+        def load_scales(queues, plane, scales):
+            for quad, queue in enumerate(queues):
                 queue.dma_start(
                     out=plane[32 * quad : 32 * quad + 4, :].bitcast(I32),
                     in_=scales[0, 4 * quad : 4 * quad + 4, :].bitcast(I32),
                 )
 
-        load_scales(nc.scalar, tags_plane, tags_scales)
         raw2 = sb.tile([P, PACK, Q], F32, name="raw2")
         raw1 = sb.tile([P, PACK, Q], F32, name="raw1")
         nc.sync.dma_start(out=raw2[:], in_=query2.rearrange("(p j) w -> p j w", j=PACK))
+        load_scales((nc.scalar, nc.sync, nc.scalar, nc.sync), tags_plane, tags_scales)
         tags = sb.tile([P, 2 * T], U8, name="tags", align_bytes=64)
         nc.sync.dma_start(out=tags[:].bitcast(I32), in_=tags_words[0].bitcast(I32))
         nc.sync.dma_start(out=raw1[:], in_=query.rearrange("(p j) w -> p j w", j=PACK))
         keys_flat = keys_words[0].rearrange("p n t -> p (n t)")
         keys = sb.tile([P, T], U32, name="keys", align_bytes=64)
         nc.sync.dma_start(out=keys[:].bitcast(I32), in_=keys_flat.bitcast(I32))
-        load_scales(nc.sync, keys_plane, keys_scales)
+        load_scales((nc.sync,) * 4, keys_plane, keys_scales)
         list1 = sb.tile([P, LIST_COLS], U16, name="list1")
         list2 = sb.tile([P, LIST_COLS], U16, name="list2")
         list3 = sb.tile([P, LIST_COLS], U16, name="list3")

@@ -25,6 +25,7 @@ HALF_T = T // 2
 HALF_I = I // 2
 LIST_COLS = I // 16
 HALF_LIST = LIST_COLS // 2
+SUM_RUNS = ((768, 1024), (0, 384), (384, 768))
 TOKEN_RUNS = ((0, 512), (512, 768), (768, 896), (896, 1024))
 
 
@@ -54,9 +55,10 @@ def tile_attend_swapped_parts_kernel(
         nc.sync.dma_start(out=tags[:].bitcast(I32), in_=tags_words[0].bitcast(I32))
         nc.sync.dma_start(out=raw1[:], in_=query.rearrange("(p j) w -> p j w", j=PACK))
         keys_flat = keys_words[0].rearrange("p n t -> p (n t)")
-        keys = sb.tile([P, T], U32, name="keys", align_bytes=64)
-        nc.sync.dma_start(out=keys[:].bitcast(I32), in_=keys_flat.bitcast(I32))
+        keys = [sb.tile([P, HALF_T], U32, name="keys%d" % h, align_bytes=64) for h in range(2)]
+        nc.sync.dma_start(out=keys[0][:].bitcast(I32), in_=keys_flat[:, : 4 * HALF_T].bitcast(I32))
         load_scales((nc.sync,) * 4, keys_plane, keys_scales)
+        nc.sync.dma_start(out=keys[1][:].bitcast(I32), in_=keys_flat[:, 4 * HALF_T :].bitcast(I32))
         list1 = sb.tile([P, LIST_COLS], U16, name="list1")
         list2 = sb.tile([P, LIST_COLS], U16, name="list2")
         list3 = sb.tile([P, LIST_COLS], U16, name="list3")
@@ -102,7 +104,7 @@ def tile_attend_swapped_parts_kernel(
                 out=bank[:],
                 lhsT=codes1[:].bitcast(FP8X4),
                 lhsT_scale=plane1[:],
-                rhs=keys[:, lo:hi].bitcast(FP8X4),
+                rhs=keys[lo // HALF_T][:, lo % HALF_T : lo % HALF_T + hi - lo].bitcast(FP8X4),
                 rhs_scale=keys_plane[:, lo:hi],
                 start=False,
                 stop=True,
@@ -114,15 +116,17 @@ def tile_attend_swapped_parts_kernel(
 
         ident = sb.tile([P, P], F32, name="ident")
         make_identity(nc, ident[:])
-        turned = [ps.tile([P, HALF_T], F32, name="turned%d" % h) for h in range(2)]
-        turned_sb = []
-        for h in range(2):
-            for b in range(4):
-                col = h * HALF_T + b * P
-                nc.tensor.matmul(
-                    turned[h][:, b * P : (b + 1) * P], a[:, col : col + P], ident[:],
-                    start=(b == 0), stop=False, is_transpose=True,
-                )
+        turned = [ps.tile([P, hi - lo], F32, name="turned%d" % lo) for lo, hi in SUM_RUNS]
+
+        def add_turned(source, first, last):
+            for bank, (lo, hi) in zip(turned, SUM_RUNS):
+                for col in range(lo, hi, P):
+                    nc.tensor.matmul(
+                        bank[:, col - lo : col - lo + P], source[:, col : col + P], ident[:],
+                        start=(first and col == lo), stop=(last and col == hi - P), is_transpose=True,
+                    )
+
+        add_turned(a, True, False)
 
         at2 = sb.tile([P, I], F32, name="at2")
         minus_at1 = sb.tile([P, I], F32, name="minus_at1")
@@ -136,32 +140,21 @@ def tile_attend_swapped_parts_kernel(
         nc.vector.tensor_tensor(f1[1][:].indirect(list1[:, l1]), at2[:, s1], minus_at1[:, s1], ADD)
         nc.vector.tensor_tensor(f2[:].indirect(list2[:]), at2[:], minus_at1[:], ADD)
 
-        c1 = [ps.tile([P, HALF_T], F32, name="c1_%d" % h) for h in range(2)]
-        for h in range(2):
-            for b in range(4):
-                col = h * HALF_T + b * P
-                nc.tensor.matmul(
-                    turned[h][:, b * P : (b + 1) * P], f1[0][:, col : col + P], ident[:],
-                    start=False, stop=False, is_transpose=True,
-                )
-        for h in range(2):
-            for b in range(4):
-                col = h * HALF_T + b * P
-                nc.tensor.matmul(
-                    turned[h][:, b * P : (b + 1) * P], f1[1][:, col : col + P], ident[:],
-                    start=False, stop=(b == 3), is_transpose=True,
-                )
-            c1_turned = sb.tile([P, HALF_T], F32, name="c1_turned%d" % h)
-            nc.scalar.copy(out=c1_turned[:], in_=turned[h][:])
-            turned_sb.append(c1_turned)
-        for h in range(2):
-            for b in range(4):
-                nc.tensor.transpose(c1[h][:, b * P : (b + 1) * P], turned_sb[h][:, b * P : (b + 1) * P], ident[:])
-
+        add_turned(f1[0], False, False)
+        add_turned(f1[1], False, True)
         c2 = sb.tile([P, T], F32, name="c2")
-        for h in range(2):
-            cols = slice(h * HALF_T, (h + 1) * HALF_T)
-            nc.vector.tensor_tensor(c2[:, cols], c1[h][:], f2[:, cols], SUB)
+        for run, (lo, hi) in enumerate(SUM_RUNS):
+            c1_turned = sb.tile([P, hi - lo], F32, name="c1_turned%d" % lo)
+            nc.scalar.copy(out=c1_turned[:], in_=turned[run][:])
+            c1 = ps.tile([P, hi - lo], F32, name="c1_%d" % lo, tag="bank%d" % TOKEN_RUNS[run][0])
+            for col in range(0, hi - lo, P):
+                nc.tensor.transpose(c1[:, col : col + P], c1_turned[:, col : col + P], ident[:])
+            if run == 0:
+                c1_sb = sb.tile([P, hi - lo], F32, name="c1_sb")
+                nc.scalar.copy(out=c1_sb[:], in_=c1[:])
+                nc.gpsimd.tensor_tensor(c2[:, lo:hi], c1_sb[:], f2[:, lo:hi], SUB)
+            else:
+                nc.vector.tensor_tensor(c2[:, lo:hi], c1[:], f2[:, lo:hi], SUB)
 
         res0 = sb.tile([P, HALF_I], F32, name="res0")
         res1 = sb.tile([P, HALF_I], F32, name="res1")

@@ -55,10 +55,9 @@ def tile_attend_swapped_parts_kernel(
         nc.sync.dma_start(out=tags[:].bitcast(I32), in_=tags_words[0].bitcast(I32))
         nc.sync.dma_start(out=raw1[:], in_=query.rearrange("(p j) w -> p j w", j=PACK))
         keys_flat = keys_words[0].rearrange("p n t -> p (n t)")
-        keys = [sb.tile([P, HALF_T], U32, name="keys%d" % h, align_bytes=64) for h in range(2)]
-        nc.sync.dma_start(out=keys[0][:].bitcast(I32), in_=keys_flat[:, : 4 * HALF_T].bitcast(I32))
+        keys = sb.tile([P, T], U32, name="keys", align_bytes=64)
+        nc.sync.dma_start(out=keys[:].bitcast(I32), in_=keys_flat.bitcast(I32))
         load_scales((nc.sync,) * 4, keys_plane, keys_scales)
-        nc.sync.dma_start(out=keys[1][:].bitcast(I32), in_=keys_flat[:, 4 * HALF_T :].bitcast(I32))
         list1 = sb.tile([P, LIST_COLS], U16, name="list1")
         list2 = sb.tile([P, LIST_COLS], U16, name="list2")
         list3 = sb.tile([P, LIST_COLS], U16, name="list3")
@@ -104,7 +103,7 @@ def tile_attend_swapped_parts_kernel(
                 out=bank[:],
                 lhsT=codes1[:].bitcast(FP8X4),
                 lhsT_scale=plane1[:],
-                rhs=keys[lo // HALF_T][:, lo % HALF_T : lo % HALF_T + hi - lo].bitcast(FP8X4),
+                rhs=keys[:, lo:hi].bitcast(FP8X4),
                 rhs_scale=keys_plane[:, lo:hi],
                 start=False,
                 stop=True,

from contextlib import ExitStack

import concourse.mybir as mybir
from concourse.masks import make_identity

D, T, I, Q = 512, 1024, 512, 128
FLOPS = 2 * 2 * D * Q * T

F32 = mybir.dt.float32
BF16 = mybir.dt.bfloat16
I32 = mybir.dt.int32
U32 = mybir.dt.uint32
U16 = mybir.dt.uint16
U8 = mybir.dt.uint8
FP8X4 = mybir.dt.float8_e4m3fn_x4
FP4X4 = mybir.dt.float4_e2m1fn_x4
ADD = mybir.AluOpType.add
SUB = mybir.AluOpType.subtract
MULT = mybir.AluOpType.mult
COPY = mybir.ActivationFunctionType.Copy

P = 128
PACK = 4
HALF_T = T // 2
HALF_I = I // 2
LIST_COLS = I // 16
HALF_LIST = LIST_COLS // 2
SUM_RUNS = ((768, 1024), (0, 384), (384, 768))
TOKEN_RUNS = ((0, 512), (512, 768), (768, 896), (896, 1024))


def tile_attend_swapped_parts_kernel(
    tc, query, query2, keys_words, keys_scales, tags_words, tags_scales, offs, offs2, offs3, out
):
    nc = tc.nc
    with ExitStack() as ctx:
        sb = ctx.enter_context(tc.tile_pool(name="sb", bufs=1))
        ps = ctx.enter_context(tc.psum_pool(name="ps", bufs=1))

        tags_plane = sb.tile([P, T], U8, name="tags_plane", align_bytes=64)
        keys_plane = sb.tile([P, T], U8, name="keys_plane", align_bytes=64)

        def load_scales(queues, plane, scales):
            for quad, queue in enumerate(queues):
                queue.dma_start(
                    out=plane[32 * quad : 32 * quad + 4, :].bitcast(I32),
                    in_=scales[0, 4 * quad : 4 * quad + 4, :].bitcast(I32),
                )

        raw2 = sb.tile([P, PACK, Q], F32, name="raw2")
        raw1 = sb.tile([P, PACK, Q], F32, name="raw1")
        nc.sync.dma_start(out=raw2[:], in_=query2.rearrange("(p j) w -> p j w", j=PACK))
        load_scales((nc.scalar, nc.sync, nc.scalar, nc.sync), tags_plane, tags_scales)
        tags = sb.tile([P, 2 * T], U8, name="tags", align_bytes=64)
        nc.sync.dma_start(out=tags[:].bitcast(I32), in_=tags_words[0].bitcast(I32))
        nc.sync.dma_start(out=raw1[:], in_=query.rearrange("(p j) w -> p j w", j=PACK))
        keys_flat = keys_words[0].rearrange("p n t -> p (n t)")
        keys = sb.tile([P, T], U32, name="keys", align_bytes=64)
        nc.sync.dma_start(out=keys[:].bitcast(I32), in_=keys_flat.bitcast(I32))
        load_scales((nc.sync,) * 4, keys_plane, keys_scales)
        list1 = sb.tile([P, LIST_COLS], U16, name="list1")
        list2 = sb.tile([P, LIST_COLS], U16, name="list2")
        list3 = sb.tile([P, LIST_COLS], U16, name="list3")
        nc.sync.dma_start(list1[:], offs)
        nc.sync.dma_start(list2[:], offs2)
        nc.sync.dma_start(list3[:], offs3)

        f1 = [sb.tile([P, T], F32, name="f1_%d" % s) for s in range(2)]
        for part in f1:
            nc.vector.memset(part[:], 0.0)

        grouped2 = sb.tile([P, Q, PACK], BF16, name="grouped2", align_bytes=64)
        grouped1 = sb.tile([P, Q, PACK], BF16, name="grouped1", tag="grouped1_f2", align_bytes=64)
        codes2 = sb.tile([P, Q], U32, name="codes2", align_bytes=64)
        codes1 = sb.tile([P, Q], U32, name="codes1", align_bytes=64)
        plane2 = sb.tile([P, Q], U8, name="plane2", align_bytes=64)
        plane1 = sb.tile([P, Q], U8, name="plane1", align_bytes=64)
        for raw, grouped, codes, plane in ((raw2, grouped2, codes2, plane2), (raw1, grouped1, codes1, plane1)):
            nc.vector.tensor_copy(out=grouped[:], in_=raw[:].rearrange("p j w -> p w j"))
            nc.vector.quantize_mx(
                out=codes[:].bitcast(FP8X4),
                scales=plane[:],
                in_=grouped[:].rearrange("p w j -> p (w j)"),
            )

        f2 = sb.tile([P, T], F32, name="f2", tag="grouped1_f2", align_bytes=64)
        nc.vector.memset(f2[:], 0.0)

        banks = [ps.tile([P, hi - lo], F32, name="bank%d" % lo) for lo, hi in TOKEN_RUNS]
        for bank, (lo, hi) in zip(banks, TOKEN_RUNS):
            nc.tensor.matmul_mx(
                out=bank[:],
                lhsT=codes2[:].bitcast(FP8X4),
                lhsT_scale=plane2[:],
                rhs=tags[:, 2 * lo : 2 * hi].bitcast(FP4X4),
                rhs_scale=tags_plane[:, lo:hi],
                start=True,
                stop=False,
            )
        a = sb.tile([P, T], F32, name="a")
        for run, (bank, (lo, hi)) in enumerate(zip(banks, TOKEN_RUNS)):
            nc.tensor.matmul_mx(
                out=bank[:],
                lhsT=codes1[:].bitcast(FP8X4),
                lhsT_scale=plane1[:],
                rhs=keys[:, lo:hi].bitcast(FP8X4),
                rhs_scale=keys_plane[:, lo:hi],
                start=False,
                stop=True,
            )
            if run % 2 == 0:
                nc.scalar.copy(out=a[:, lo:hi], in_=bank[:])
            else:
                nc.vector.tensor_copy(out=a[:, lo:hi], in_=bank[:])

        ident = sb.tile([P, P], F32, name="ident")
        make_identity(nc, ident[:])
        turned = [ps.tile([P, hi - lo], F32, name="turned%d" % lo) for lo, hi in SUM_RUNS]

        def add_turned(source, first, last):
            for bank, (lo, hi) in zip(turned, SUM_RUNS):
                for col in range(lo, hi, P):
                    nc.tensor.matmul(
                        bank[:, col - lo : col - lo + P], source[:, col : col + P], ident[:],
                        start=(first and col == lo), stop=(last and col == hi - P), is_transpose=True,
                    )

        add_turned(a, True, False)

        at2 = sb.tile([P, I], F32, name="at2")
        minus_at1 = sb.tile([P, I], F32, name="minus_at1")
        s0, s1 = slice(0, HALF_I), slice(HALF_I, I)
        l0, l1 = slice(0, HALF_LIST), slice(HALF_LIST, LIST_COLS)
        nc.vector.tensor_scalar(minus_at1[:, s0], a[:].indirect(list1[:, l0]), -1.0, 0.0, MULT, ADD)
        nc.scalar.activation(at2[:, s0], a[:].indirect(list2[:, l0]), COPY)
        nc.vector.tensor_tensor(f1[0][:].indirect(list1[:, l0]), at2[:, s0], minus_at1[:, s0], ADD)
        nc.scalar.activation(at2[:, s1], a[:].indirect(list2[:, l1]), COPY)
        nc.scalar.activation(minus_at1[:, s1], a[:].indirect(list1[:, l1]), COPY, scale=-1.0)
        nc.vector.tensor_tensor(f1[1][:].indirect(list1[:, l1]), at2[:, s1], minus_at1[:, s1], ADD)
        nc.vector.tensor_tensor(f2[:].indirect(list2[:]), at2[:], minus_at1[:], ADD)

        add_turned(f1[0], False, False)
        add_turned(f1[1], False, True)
        c2 = sb.tile([P, T], F32, name="c2")
        for run, (lo, hi) in enumerate(SUM_RUNS):
            c1_turned = sb.tile([P, hi - lo], F32, name="c1_turned%d" % lo)
            nc.scalar.copy(out=c1_turned[:], in_=turned[run][:])
            c1 = ps.tile([P, hi - lo], F32, name="c1_%d" % lo, tag="bank%d" % TOKEN_RUNS[run][0])
            for col in range(0, hi - lo, P):
                nc.tensor.transpose(c1[:, col : col + P], c1_turned[:, col : col + P], ident[:])
            if run == 0:
                c1_sb = sb.tile([P, hi - lo], F32, name="c1_sb")
                nc.scalar.copy(out=c1_sb[:], in_=c1[:])
                nc.gpsimd.tensor_tensor(c2[:, lo:hi], c1_sb[:], f2[:, lo:hi], SUB)
            else:
                nc.vector.tensor_tensor(c2[:, lo:hi], c1[:], f2[:, lo:hi], SUB)

        res0 = sb.tile([P, HALF_I], F32, name="res0")
        res1 = sb.tile([P, HALF_I], F32, name="res1")
        nc.vector.tensor_copy(res0[:], c2[:].indirect(list3[:, l0]))
        nc.scalar.activation(res1[:], c2[:].indirect(list3[:, l1]), COPY)
        nc.sync.dma_start(out=out[:, s0], in_=res0[:])
        nc.scalar.dma_start(out=out[:, s1], in_=res1[:])
